import numpy as np
import ml_dtypes


def mxq(x, axis, fmt="e4m3"):
    dtype, down = {"e4m3": (ml_dtypes.float8_e4m3fn, 7), "e5m2": (ml_dtypes.float8_e5m2, 14)}[fmt]
    v = np.moveaxis(np.asarray(x, np.float32).astype(ml_dtypes.bfloat16).astype(np.float64), axis, -1)
    blocks = v.reshape(v.shape[:-1] + (-1, 32))
    amax = np.abs(blocks).max(-1, keepdims=True)
    byte = np.maximum(np.where(amax > 0, np.frexp(amax)[1] - 1 + 127, 0) - down, 1)
    scale = np.exp2(byte - 127.0)
    codes = (blocks / scale).astype(np.float32).astype(dtype).astype(np.float64)
    return np.moveaxis((codes * scale).reshape(v.shape), -1, axis)


WIDE = False


def mx_kscale(k):
    if not WIDE:
        return np.ones(k)
    levels = np.array([10, -10, 5, -5, 0])
    if k % 512:
        return np.exp2(np.random.permutation(np.resize(levels, k // 32))).repeat(32)
    a = np.empty((k // 512, 16))
    for p in range(k // 512):
        a[p, :8] = np.random.permutation(np.resize(levels, 8))
        for g in range(8):
            far = levels[np.abs(levels - a[p, g]) >= 10]
            a[p, g + 8] = far[np.random.randint(len(far))]
    return np.exp2(a.ravel()).repeat(32)


def f64(x):
    return np.asarray(x).astype(np.float64)


def striped(idx):
    return np.tile(idx.reshape(-1, 16).T, (8, 1)).astype(np.uint16)


def unstriped(offs):
    return offs[:16].T.reshape(-1).astype(np.int64)


def pack_weight(w):
    k, n = w.shape
    w = f64(np.asarray(w, np.float32).astype(ml_dtypes.bfloat16)).reshape(k // 32, 32, n)
    amax = np.abs(w).max(1)
    byte = np.clip(np.where(amax > 0, np.frexp(amax)[1] - 1 + 127 - 7, 1), 1, 254)
    scaled = (w * np.exp2(127.0 - byte)[:, None, :]).reshape(k, n).astype(np.float32)
    words = np.ascontiguousarray(scaled.reshape(k // 512, 128, 4, n).transpose(0, 1, 3, 2)).astype(ml_dtypes.float8_e4m3fn).view(np.uint8)
    return words, np.ascontiguousarray(byte.astype(np.uint8).reshape(k // 512, 16, n))


def unpack_weight(words, scales):
    g, p, n, _ = words.shape
    vals = np.ascontiguousarray(words).view(ml_dtypes.float8_e4m3fn).astype(np.float64) * np.repeat(np.exp2(scales.astype(np.float64) - 127.0), 8, axis=1)[..., None]
    return vals.transpose(0, 1, 3, 2).reshape(g * 512, n)


E2M1 = np.array([0.0, 0.5, 1.0, 1.5, 2.0, 3.0, 4.0, 6.0, -0.0, -0.5, -1.0, -1.5, -2.0, -3.0, -4.0, -6.0])


def pack_fp4(w):
    k, n = w.shape
    w = f64(np.asarray(w, np.float32).astype(ml_dtypes.bfloat16)).reshape(k // 32, 32, n)
    amax = np.abs(w).max(1)
    mant, ex = np.frexp(amax / 6.0)
    byte = np.clip(np.where(amax > 0, np.where(mant > 0.5, ex, ex - 1) + 127, 1), 1, 254)
    scaled = (w * np.exp2(127.0 - byte)[:, None, :]).reshape(k, n).astype(np.float32)
    c = np.ascontiguousarray(scaled.reshape(k // 512, 128, 4, n).transpose(0, 1, 3, 2)).astype(ml_dtypes.float4_e2m1fn).view(np.uint8) & 0xF
    words = (c[..., 0::2] | (c[..., 1::2] << 4)).reshape(k // 512, 128, 2 * n)
    return np.ascontiguousarray(words), np.ascontiguousarray(byte.astype(np.uint8).reshape(k // 512, 16, n))


def unpack_fp4(words, scales):
    g, _, n = scales.shape
    words = np.ascontiguousarray(words).reshape(g, 128, n, 2)
    nib = np.empty((g, 128, n, 4), np.uint8)
    nib[..., 0::2] = words & 0xF
    nib[..., 1::2] = words >> 4
    vals = E2M1[nib] * np.repeat(np.exp2(scales.astype(np.float64) - 127.0), 8, axis=1)[..., None]
    return vals.transpose(0, 1, 3, 2).reshape(g * 512, n)


def planes(y):
    n, m = y.shape
    v = y.astype(np.float32).astype(ml_dtypes.bfloat16).astype(np.float64).reshape(n // 32, 32, m)
    top = np.abs(v).max(1)
    byte = np.clip(np.where(top > 0, np.frexp(top)[1] - 1 + 127 - 7, 1), 1, 254)
    codes = (v * np.exp2(127.0 - byte)[:, None, :]).reshape(n, m).astype(np.float32).astype(ml_dtypes.float8_e4m3fn).view(np.uint8)
    words = codes.reshape(n // 512, 128, 4, m).transpose(0, 1, 3, 2)
    return np.ascontiguousarray(words), np.ascontiguousarray(byte.astype(np.uint8).reshape(n // 512, 16, m))


K, T, S, N, H, U = 512, 2048, 512, 512, 512, 1024


def setup_inputs():
    n = np.random.standard_normal
    s = mx_kscale(K)[:, None]
    u = mx_kscale(H)
    packed_xT = pack_weight(n((K, T)) * s)
    packed_w1 = pack_fp4(n((K, N)) / np.sqrt(K) / s)
    packed_w2 = pack_fp4(n((K, N)) / np.sqrt(K) / s)
    packed_w3 = pack_fp4(n((H, N)) / np.sqrt(H) / u[:, None])
    return {
        "x_words": packed_xT[0],
        "x_scales": packed_xT[1],
        "w1_words": packed_w1[0],
        "w1_scales": packed_w1[1],
        "w2_words": packed_w2[0],
        "w2_scales": packed_w2[1],
        "unit": (np.random.uniform(0.6, 1.4, (H, 1)) * u[:, None]).astype(np.float32),
        "w3_words": packed_w3[0],
        "w3_scales": packed_w3[1],
        "offs": striped(np.random.permutation(T)[:S]),
        "fa": striped(np.random.permutation(np.concatenate([np.arange(S), np.random.randint(0, S, U - S)]))),
        "fb": striped(np.random.permutation(np.concatenate([np.arange(S), np.random.randint(0, S, U - S)]))),
    }


def reference(x_words, x_scales, w1_words, w1_scales, w2_words, w2_scales, unit, w3_words, w3_scales, offs, fa, fb):
    xq = unpack_weight(x_words, x_scales)[:, unstriped(offs)]
    y = unpack_fp4(w1_words, w1_scales).T @ xq
    ya = y[:, unstriped(fa)]
    yb_ = y[:, unstriped(fb)]
    dy = ya - yb_
    z1 = unpack_fp4(w2_words, w2_scales).T @ xq
    za = z1[:, unstriped(fa)]
    zb_ = z1[:, unstriped(fb)]
    dz_ = za - zb_
    hid = f64(unit) * (dy * dz_)
    out_0 = unpack_fp4(w3_words, w3_scales).T @ mxq(hid, 0, "e4m3")
    return (out_0,) + planes(out_0)

@@ -1,0 +1,177 @@
+from contextlib import ExitStack
+
+import concourse.mybir as mybir
+
+F32 = mybir.dt.float32
+BF16 = mybir.dt.bfloat16
+I32 = mybir.dt.int32
+U32 = mybir.dt.uint32
+U16 = mybir.dt.uint16
+U8 = mybir.dt.uint8
+FP8X4 = mybir.dt.float8_e4m3fn_x4
+FP4X4 = mybir.dt.float4_e2m1fn_x4
+COPY = mybir.ActivationFunctionType.Copy
+ADD = mybir.AluOpType.add
+MULT = mybir.AluOpType.mult
+
+P = 128
+PACK = 4
+T, S, N, U = 2048, 512, 512, 1024
+SPARE = 8
+BANK = 512
+CHUNKS = (512, 384, 128)
+
+PASSES = {512: ((0, 512),), 384: ((0, 256), (256, 384)), 256: ((0, 256),), 128: ((0, 128),)}
+
+FLOPS = 2 * 512 * 512 * (512 + 512 + 1024)
+
+
+def tile_picked_yfairsp_mul_po_kernel(
+    tc, x_words, x_scales, w1_words, w1_scales, w2_words, w2_scales, unit, w3_words, w3_scales,
+    offs, fa, fb, out_0, out_1, out_2,
+):
+    nc = tc.nc
+    with ExitStack() as ctx:
+        keep = ctx.enter_context(tc.tile_pool(name="keep", bufs=1))
+        psum = ctx.enter_context(tc.psum_pool(name="psum", bufs=8))
+
+        def load_scale_rows(queue, plane, rows):
+            for q in range(4):
+                queue.dma_start(out=plane[32 * q : 32 * q + 4, :].bitcast(I32), in_=rows[0, 4 * q : 4 * q + 4, :].bitcast(I32))
+
+        offs_sb = keep.tile([P, S // 16], U16, name="offs_sb")
+        fa_sb = keep.tile([P, U // 16], U16, name="fa_sb")
+        fb_sb = keep.tile([P, U // 16], U16, name="fb_sb")
+        xw = keep.tile([P, T], U32, name="xw", align_bytes=64)
+        xs = keep.tile([P, T], U8, name="xs", align_bytes=64)
+        w_raw = [keep.tile([P, 2 * N], U8, name="w_raw%d" % i, align_bytes=64) for i in range(2)]
+        s_raw = [keep.tile([P, N], U8, name="s_raw%d" % i, align_bytes=64) for i in range(2)]
+        w_dealt = [keep.tile([P, 2 * N], U8, name="w_dealt%d" % i, align_bytes=64) for i in range(3)]
+        s_dealt = [keep.tile([P, N], U8, name="s_dealt%d" % i, align_bytes=64) for i in range(3)]
+        unit_sb = keep.tile([P, PACK], F32, name="unit_sb")
+        ywin = [keep.tile([P, S + SPARE], F32, name="ywin%d" % t) for t in range(PACK)]
+        zwin = [keep.tile([P, S + SPARE], F32, name="zwin%d" % t) for t in range(PACK)]
+
+        nc.vector.memset(xs[:].bitcast(I32), 0)
+        nc.gpsimd.memset(s_raw[0][:].bitcast(I32), 0)
+        nc.gpsimd.memset(s_raw[1][:].bitcast(I32), 0)
+        nc.gpsimd.dma_start(out=unit_sb[:], in_=unit.rearrange("(p t) o -> p (t o)", t=PACK))
+        for t in range(PACK):
+            nc.vector.memset(ywin[t][:, S:], 0.0)
+            nc.vector.memset(zwin[t][:, S:], 0.0)
+
+        nc.sync.dma_start(offs_sb[:], offs)
+        nc.scalar.dma_start(out=w_raw[0][:].bitcast(I32), in_=w1_words[0].bitcast(I32))
+        nc.sync.dma_start(fb_sb[:], fb)
+        nc.scalar.dma_start(out=w_raw[1][:].bitcast(I32), in_=w2_words[0].bitcast(I32))
+        nc.sync.dma_start(fa_sb[:], fa)
+        nc.sync.dma_start(out=xw[:].bitcast(I32), in_=x_words[0].rearrange("p n t -> p (n t)").bitcast(I32))
+        load_scale_rows(nc.sync, xs, x_scales)
+        load_scale_rows(nc.sync, s_raw[0], w1_scales)
+        load_scale_rows(nc.sync, s_raw[1], w2_scales)
+
+        def deal_words(i):
+            nc.vector.tensor_copy(
+                out=w_dealt[i][:].rearrange("p (t m b) -> p t m b", t=PACK, b=2),
+                in_=w_raw[i % 2][:].rearrange("p (m t b) -> p t m b", t=PACK, b=2),
+            )
+
+        def deal_scales(i):
+            nc.vector.tensor_copy(
+                out=s_dealt[i][:].rearrange("p (t m) -> p t m", t=PACK),
+                in_=s_raw[i % 2][:].rearrange("p (m t) -> p t m", t=PACK),
+            )
+
+        def product(out, i, t, codes, scales):
+            nc.tensor.matmul_mx(
+                out=out,
+                lhsT=w_dealt[i][:, 2 * P * t : 2 * P * (t + 1)].bitcast(FP4X4),
+                lhsT_scale=s_dealt[i][:, P * t : P * (t + 1)],
+                rhs=codes.bitcast(FP8X4),
+                rhs_scale=scales,
+                start=True,
+                stop=True,
+            )
+
+        xq = keep.tile([P, S], U32, name="xq", align_bytes=64)
+        xqs = keep.tile([P, S], U8, name="xqs", align_bytes=64)
+        deal_words(0)
+        deal_words(1)
+        nc.vector.tensor_copy(xqs[:], xs[:].indirect(offs_sb[:]))
+        nc.vector.tensor_copy(xq[:], xw[:].indirect(offs_sb[:]))
+        deal_scales(0)
+        deal_scales(1)
+        nc.sync.dma_start(out=w_raw[0][:].bitcast(I32), in_=w3_words[0].bitcast(I32))
+        load_scale_rows(nc.sync, s_raw[0], w3_scales)
+
+        for t in range(PACK):
+            ybank = psum.tile([P, BANK], F32, name="ybank", tag="bank")
+            product(ybank[:], 0, t, xq[:], xqs[:])
+            zbank = psum.tile([P, BANK], F32, name="zbank", tag="bank")
+            product(zbank[:], 1, t, xq[:], xqs[:])
+            if t != 1:
+                nc.scalar.activation(ywin[t][:, :S], ybank[:], COPY, scale=unit_sb[:, t : t + 1])
+            else:
+                nc.vector.tensor_scalar_mul(ywin[t][:, :S], ybank[:], unit_sb[:, t : t + 1])
+            if t < 2:
+                nc.vector.tensor_copy(zwin[t][:, :S], zbank[:])
+            else:
+                nc.scalar.copy(zwin[t][:, :S], zbank[:])
+        deal_words(2)
+        deal_scales(2)
+
+        out_scales = keep.tile([P, U], U8, name="out_scales", align_bytes=64)
+        out_rows = out_0.rearrange("(p t) c -> p t c", t=PACK)
+        out_words = out_1[0].rearrange("p n t -> p (n t)").bitcast(I32)
+
+        def gaps(c0, n):
+            lst = slice(c0 // 16, (c0 + n) // 16)
+            dy = keep.tile([P, PACK, n], F32, name="dy%d" % c0)
+            dz = keep.tile([P, PACK, n], F32, name="dz%d" % c0)
+            for t in range(PACK):
+                for win, gap, nm in ((ywin[t], dy, "y"), (zwin[t], dz, "z")):
+                    neg = keep.tile([P, n], F32, name="neg%s%d_%d" % (nm, t, c0))
+                    nc.scalar.activation(neg[:], win[:].indirect(fb_sb[:, lst]), COPY, scale=-1.0)
+                    nc.vector.tensor_tensor(gap[:, t, :], win[:].indirect(fa_sb[:, lst]), neg[:], ADD)
+            return dy, dz
+
+        def finish(c0, n, dy, dz):
+            hid = keep.tile([P, n, PACK], BF16, name="hid%d" % c0, align_bytes=64)
+            nc.vector.tensor_tensor(
+                hid[:].rearrange("p (c i) t -> p c t i", i=4),
+                dy[:].rearrange("p t (c i) -> p c t i", i=4),
+                dz[:].rearrange("p t (c i) -> p c t i", i=4),
+                MULT,
+            )
+            hq = keep.tile([P, n], U32, name="hq%d" % c0, align_bytes=64)
+            hs = keep.tile([P, n], U8, name="hs%d" % c0, align_bytes=64)
+            nc.vector.quantize_mx(out=hq[:].bitcast(FP8X4), scales=hs[:], in_=hid[:].rearrange("p c t -> p (c t)"))
+            res = keep.tile([P, PACK, n], F32, name="res%d" % c0)
+            per_bank = BANK // n
+            for t0 in range(0, PACK, per_bank):
+                obank = psum.tile([P, per_bank, n], F32, name="obank", tag="bank")
+                for j in range(per_bank):
+                    for a, b in PASSES[n]:
+                        product(obank[:, j, a:b], 2, t0 + j, hq[:, a:b], hs[:, a:b])
+                nc.scalar.copy(res[:, t0 : t0 + per_bank, :], obank[:])
+            nc.sync.dma_start(out=out_rows[:, :, c0 : c0 + n], in_=res[:])
+            rounded = keep.tile([P, n, PACK], BF16, name="rounded%d" % c0, align_bytes=64)
+            (nc.scalar.copy if c0 == 0 else nc.vector.tensor_copy)(
+                out=rounded[:].rearrange("p (c i) t -> p c t i", i=4),
+                in_=res[:].rearrange("p t (c i) -> p c t i", i=4),
+            )
+            oq = keep.tile([P, n], U32, name="oq%d" % c0, align_bytes=64)
+            nc.vector.quantize_mx(
+                out=oq[:].bitcast(FP8X4), scales=out_scales[:, c0 : c0 + n], in_=rounded[:].rearrange("p c t -> p (c t)")
+            )
+            nc.sync.dma_start(out=out_words[:, c0 : c0 + n], in_=oq[:].bitcast(I32))
+
+        c0 = 0
+        for n in CHUNKS:
+            dy, dz = gaps(c0, n)
+            finish(c0, n, dy, dz)
+            c0 = c0 + n
+
+        for q in range(4):
+            queue = nc.sync if q % 2 == 0 else nc.scalar
+            queue.dma_start(out=out_2[0, 4 * q : 4 * q + 4, :].bitcast(I32), in_=out_scales[32 * q : 32 * q + 4, :].bitcast(I32))

@@ -12,6 +12,7 @@ FP8X4 = mybir.dt.float8_e4m3fn_x4
 FP4X4 = mybir.dt.float4_e2m1fn_x4
 COPY = mybir.ActivationFunctionType.Copy
 ADD = mybir.AluOpType.add
+SUBTRACT = mybir.AluOpType.subtract
 MULT = mybir.AluOpType.mult
 
 P = 128
@@ -52,34 +53,34 @@ def tile_picked_yfairsp_mul_po_kernel(
         ywin = [keep.tile([P, S + SPARE], F32, name="ywin%d" % t) for t in range(PACK)]
         zwin = [keep.tile([P, S + SPARE], F32, name="zwin%d" % t) for t in range(PACK)]
 
-        nc.vector.memset(xs[:].bitcast(I32), 0)
-        nc.gpsimd.memset(s_raw[0][:].bitcast(I32), 0)
-        nc.gpsimd.memset(s_raw[1][:].bitcast(I32), 0)
+        nc.gpsimd.memset(xs[:].bitcast(I32), 0)
+        nc.vector.memset(s_raw[0][:].bitcast(I32), 0)
+        nc.vector.memset(s_raw[1][:].bitcast(I32), 0)
         nc.gpsimd.dma_start(out=unit_sb[:], in_=unit.rearrange("(p t) o -> p (t o)", t=PACK))
         for t in range(PACK):
             nc.vector.memset(ywin[t][:, S:], 0.0)
             nc.vector.memset(zwin[t][:, S:], 0.0)
 
         nc.sync.dma_start(offs_sb[:], offs)
-        nc.scalar.dma_start(out=w_raw[0][:].bitcast(I32), in_=w1_words[0].bitcast(I32))
-        nc.sync.dma_start(fb_sb[:], fb)
-        nc.scalar.dma_start(out=w_raw[1][:].bitcast(I32), in_=w2_words[0].bitcast(I32))
-        nc.sync.dma_start(fa_sb[:], fa)
-        nc.sync.dma_start(out=xw[:].bitcast(I32), in_=x_words[0].rearrange("p n t -> p (n t)").bitcast(I32))
         load_scale_rows(nc.sync, xs, x_scales)
+        nc.sync.dma_start(out=w_raw[0][:].bitcast(I32), in_=w1_words[0].bitcast(I32))
+        nc.sync.dma_start(out=w_raw[1][:].bitcast(I32), in_=w2_words[0].bitcast(I32))
+        nc.sync.dma_start(out=xw[:].bitcast(I32), in_=x_words[0].rearrange("p n t -> p (n t)").bitcast(I32))
         load_scale_rows(nc.sync, s_raw[0], w1_scales)
+        nc.sync.dma_start(fb_sb[:], fb)
+        nc.sync.dma_start(fa_sb[:], fa)
         load_scale_rows(nc.sync, s_raw[1], w2_scales)
 
         def deal_words(i):
             nc.vector.tensor_copy(
-                out=w_dealt[i][:].rearrange("p (t m b) -> p t m b", t=PACK, b=2),
-                in_=w_raw[i % 2][:].rearrange("p (m t b) -> p t m b", t=PACK, b=2),
+                out=w_dealt[i][:].bitcast(U16).rearrange("p (t m) -> p t m", t=PACK),
+                in_=w_raw[i % 2][:].bitcast(U16).rearrange("p (m t) -> p t m", t=PACK),
             )
 
-        def deal_scales(i):
+        def deal_scales(i, t0, t1):
             nc.vector.tensor_copy(
-                out=s_dealt[i][:].rearrange("p (t m) -> p t m", t=PACK),
-                in_=s_raw[i % 2][:].rearrange("p (m t) -> p t m", t=PACK),
+                out=s_dealt[i][:].rearrange("p (t m) -> p t m", t=PACK)[:, t0:t1, :],
+                in_=s_raw[i % 2][:].rearrange("p (m t) -> p t m", t=PACK)[:, t0:t1, :],
             )
 
         def product(out, i, t, codes, scales):
@@ -99,26 +100,25 @@ def tile_picked_yfairsp_mul_po_kernel(
         deal_words(1)
         nc.vector.tensor_copy(xqs[:], xs[:].indirect(offs_sb[:]))
         nc.vector.tensor_copy(xq[:], xw[:].indirect(offs_sb[:]))
-        deal_scales(0)
-        deal_scales(1)
+        deal_scales(0, 0, 1)
+        deal_scales(0, 1, PACK)
         nc.sync.dma_start(out=w_raw[0][:].bitcast(I32), in_=w3_words[0].bitcast(I32))
         load_scale_rows(nc.sync, s_raw[0], w3_scales)
 
         for t in range(PACK):
             ybank = psum.tile([P, BANK], F32, name="ybank", tag="bank")
             product(ybank[:], 0, t, xq[:], xqs[:])
-            zbank = psum.tile([P, BANK], F32, name="zbank", tag="bank")
-            product(zbank[:], 1, t, xq[:], xqs[:])
-            if t != 1:
+            if t == 0:
                 nc.scalar.activation(ywin[t][:, :S], ybank[:], COPY, scale=unit_sb[:, t : t + 1])
             else:
                 nc.vector.tensor_scalar_mul(ywin[t][:, :S], ybank[:], unit_sb[:, t : t + 1])
-            if t < 2:
-                nc.vector.tensor_copy(zwin[t][:, :S], zbank[:])
-            else:
-                nc.scalar.copy(zwin[t][:, :S], zbank[:])
+        deal_scales(1, 0, PACK)
+        for t in range(PACK):
+            zbank = psum.tile([P, BANK], F32, name="zbank", tag="bank")
+            product(zbank[:], 1, t, xq[:], xqs[:])
+            (nc.scalar.copy if t >= 2 else nc.vector.tensor_copy)(zwin[t][:, :S], zbank[:])
         deal_words(2)
-        deal_scales(2)
+        deal_scales(2, 0, PACK)
 
         out_scales = keep.tile([P, U], U8, name="out_scales", align_bytes=64)
         out_rows = out_0.rearrange("(p t) c -> p t c", t=PACK)
@@ -128,11 +128,22 @@ def tile_picked_yfairsp_mul_po_kernel(
             lst = slice(c0 // 16, (c0 + n) // 16)
             dy = keep.tile([P, PACK, n], F32, name="dy%d" % c0)
             dz = keep.tile([P, PACK, n], F32, name="dz%d" % c0)
-            for t in range(PACK):
-                for win, gap, nm in ((ywin[t], dy, "y"), (zwin[t], dz, "z")):
+            last = c0 + n == U
+            if last:
+                pos = keep.tile([P, PACK, n], F32, name="pos")
+                sub = keep.tile([P, PACK, n], F32, name="sub")
+            for wins, gap, nm in ((ywin, dy, "y"), (zwin, dz, "z")):
+                for t in range(PACK):
+                    win = wins[t]
+                    if last and nm == "z":
+                        nc.scalar.activation(sub[:, t, :], win[:].indirect(fb_sb[:, lst]), COPY)
+                        nc.scalar.activation(pos[:, t, :], win[:].indirect(fa_sb[:, lst]), COPY)
+                        continue
                     neg = keep.tile([P, n], F32, name="neg%s%d_%d" % (nm, t, c0))
                     nc.scalar.activation(neg[:], win[:].indirect(fb_sb[:, lst]), COPY, scale=-1.0)
                     nc.vector.tensor_tensor(gap[:, t, :], win[:].indirect(fa_sb[:, lst]), neg[:], ADD)
+            if last:
+                nc.vector.tensor_tensor(dz[:], pos[:], sub[:], SUBTRACT)
             return dy, dz
 
         def finish(c0, n, dy, dz):

from contextlib import ExitStack

import concourse.mybir as mybir

F32 = mybir.dt.float32
BF16 = mybir.dt.bfloat16
I32 = mybir.dt.int32
U32 = mybir.dt.uint32
U16 = mybir.dt.uint16
U8 = mybir.dt.uint8
FP8X4 = mybir.dt.float8_e4m3fn_x4
FP4X4 = mybir.dt.float4_e2m1fn_x4
COPY = mybir.ActivationFunctionType.Copy
ADD = mybir.AluOpType.add
SUBTRACT = mybir.AluOpType.subtract
MULT = mybir.AluOpType.mult

P = 128
PACK = 4
T, S, N, U = 2048, 512, 512, 1024
SPARE = 8
BANK = 512
CHUNKS = (512, 384, 128)

PASSES = {512: ((0, 512),), 384: ((0, 256), (256, 384)), 256: ((0, 256),), 128: ((0, 128),)}

FLOPS = 2 * 512 * 512 * (512 + 512 + 1024)


def tile_picked_yfairsp_mul_po_kernel(
    tc, x_words, x_scales, w1_words, w1_scales, w2_words, w2_scales, unit, w3_words, w3_scales,
    offs, fa, fb, out_0, out_1, out_2,
):
    nc = tc.nc
    with ExitStack() as ctx:
        keep = ctx.enter_context(tc.tile_pool(name="keep", bufs=1))
        psum = ctx.enter_context(tc.psum_pool(name="psum", bufs=8))

        def load_scale_rows(queue, plane, rows):
            for q in range(4):
                queue.dma_start(out=plane[32 * q : 32 * q + 4, :].bitcast(I32), in_=rows[0, 4 * q : 4 * q + 4, :].bitcast(I32))

        offs_sb = keep.tile([P, S // 16], U16, name="offs_sb")
        fa_sb = keep.tile([P, U // 16], U16, name="fa_sb")
        fb_sb = keep.tile([P, U // 16], U16, name="fb_sb")
        xw = keep.tile([P, T], U32, name="xw", align_bytes=64)
        xs = keep.tile([P, T], U8, name="xs", align_bytes=64)
        w_raw = [keep.tile([P, 2 * N], U8, name="w_raw%d" % i, align_bytes=64) for i in range(2)]
        s_raw = [keep.tile([P, N], U8, name="s_raw%d" % i, align_bytes=64) for i in range(2)]
        w_dealt = [keep.tile([P, 2 * N], U8, name="w_dealt%d" % i, align_bytes=64) for i in range(3)]
        s_dealt = [keep.tile([P, N], U8, name="s_dealt%d" % i, align_bytes=64) for i in range(3)]
        unit_sb = keep.tile([P, PACK], F32, name="unit_sb")
        ywin = [keep.tile([P, S + SPARE], F32, name="ywin%d" % t) for t in range(PACK)]
        zwin = [keep.tile([P, S + SPARE], F32, name="zwin%d" % t) for t in range(PACK)]

        nc.gpsimd.memset(xs[:].bitcast(I32), 0)
        nc.vector.memset(s_raw[0][:].bitcast(I32), 0)
        nc.vector.memset(s_raw[1][:].bitcast(I32), 0)
        nc.gpsimd.dma_start(out=unit_sb[:], in_=unit.rearrange("(p t) o -> p (t o)", t=PACK))
        for t in range(PACK):
            nc.vector.memset(ywin[t][:, S:], 0.0)
            nc.vector.memset(zwin[t][:, S:], 0.0)

        nc.sync.dma_start(offs_sb[:], offs)
        load_scale_rows(nc.sync, xs, x_scales)
        nc.sync.dma_start(out=w_raw[0][:].bitcast(I32), in_=w1_words[0].bitcast(I32))
        nc.sync.dma_start(out=w_raw[1][:].bitcast(I32), in_=w2_words[0].bitcast(I32))
        nc.sync.dma_start(out=xw[:].bitcast(I32), in_=x_words[0].rearrange("p n t -> p (n t)").bitcast(I32))
        load_scale_rows(nc.sync, s_raw[0], w1_scales)
        nc.sync.dma_start(fb_sb[:], fb)
        nc.sync.dma_start(fa_sb[:], fa)
        load_scale_rows(nc.sync, s_raw[1], w2_scales)

        def deal_words(i):
            nc.vector.tensor_copy(
                out=w_dealt[i][:].bitcast(U16).rearrange("p (t m) -> p t m", t=PACK),
                in_=w_raw[i % 2][:].bitcast(U16).rearrange("p (m t) -> p t m", t=PACK),
            )

        def deal_scales(i, t0, t1):
            nc.vector.tensor_copy(
                out=s_dealt[i][:].rearrange("p (t m) -> p t m", t=PACK)[:, t0:t1, :],
                in_=s_raw[i % 2][:].rearrange("p (m t) -> p t m", t=PACK)[:, t0:t1, :],
            )

        def product(out, i, t, codes, scales):
            nc.tensor.matmul_mx(
                out=out,
                lhsT=w_dealt[i][:, 2 * P * t : 2 * P * (t + 1)].bitcast(FP4X4),
                lhsT_scale=s_dealt[i][:, P * t : P * (t + 1)],
                rhs=codes.bitcast(FP8X4),
                rhs_scale=scales,
                start=True,
                stop=True,
            )

        xq = keep.tile([P, S], U32, name="xq", align_bytes=64)
        xqs = keep.tile([P, S], U8, name="xqs", align_bytes=64)
        deal_words(0)
        deal_words(1)
        nc.vector.tensor_copy(xqs[:], xs[:].indirect(offs_sb[:]))
        nc.vector.tensor_copy(xq[:], xw[:].indirect(offs_sb[:]))
        deal_scales(0, 0, 1)
        deal_scales(0, 1, PACK)
        nc.sync.dma_start(out=w_raw[0][:].bitcast(I32), in_=w3_words[0].bitcast(I32))
        load_scale_rows(nc.sync, s_raw[0], w3_scales)

        for t in range(PACK):
            ybank = psum.tile([P, BANK], F32, name="ybank", tag="bank")
            product(ybank[:], 0, t, xq[:], xqs[:])
            if t == 0:
                nc.scalar.activation(ywin[t][:, :S], ybank[:], COPY, scale=unit_sb[:, t : t + 1])
            else:
                nc.vector.tensor_scalar_mul(ywin[t][:, :S], ybank[:], unit_sb[:, t : t + 1])
        deal_scales(1, 0, PACK)
        for t in range(PACK):
            zbank = psum.tile([P, BANK], F32, name="zbank", tag="bank")
            product(zbank[:], 1, t, xq[:], xqs[:])
            (nc.scalar.copy if t >= 2 else nc.vector.tensor_copy)(zwin[t][:, :S], zbank[:])
        deal_words(2)
        deal_scales(2, 0, PACK)

        out_scales = keep.tile([P, U], U8, name="out_scales", align_bytes=64)
        out_rows = out_0.rearrange("(p t) c -> p t c", t=PACK)
        out_words = out_1[0].rearrange("p n t -> p (n t)").bitcast(I32)

        def gaps(c0, n):
            lst = slice(c0 // 16, (c0 + n) // 16)
            dy = keep.tile([P, PACK, n], F32, name="dy%d" % c0)
            dz = keep.tile([P, PACK, n], F32, name="dz%d" % c0)
            last = c0 + n == U
            if last:
                pos = keep.tile([P, PACK, n], F32, name="pos")
                sub = keep.tile([P, PACK, n], F32, name="sub")
            for wins, gap, nm in ((ywin, dy, "y"), (zwin, dz, "z")):
                for t in range(PACK):
                    win = wins[t]
                    if last and nm == "z":
                        nc.scalar.activation(sub[:, t, :], win[:].indirect(fb_sb[:, lst]), COPY)
                        nc.scalar.activation(pos[:, t, :], win[:].indirect(fa_sb[:, lst]), COPY)
                        continue
                    neg = keep.tile([P, n], F32, name="neg%s%d_%d" % (nm, t, c0))
                    nc.scalar.activation(neg[:], win[:].indirect(fb_sb[:, lst]), COPY, scale=-1.0)
                    nc.vector.tensor_tensor(gap[:, t, :], win[:].indirect(fa_sb[:, lst]), neg[:], ADD)
            if last:
                nc.vector.tensor_tensor(dz[:], pos[:], sub[:], SUBTRACT)
            return dy, dz

        def finish(c0, n, dy, dz):
            hid = keep.tile([P, n, PACK], BF16, name="hid%d" % c0, align_bytes=64)
            nc.vector.tensor_tensor(
                hid[:].rearrange("p (c i) t -> p c t i", i=4),
                dy[:].rearrange("p t (c i) -> p c t i", i=4),
                dz[:].rearrange("p t (c i) -> p c t i", i=4),
                MULT,
            )
            hq = keep.tile([P, n], U32, name="hq%d" % c0, align_bytes=64)
            hs = keep.tile([P, n], U8, name="hs%d" % c0, align_bytes=64)
            nc.vector.quantize_mx(out=hq[:].bitcast(FP8X4), scales=hs[:], in_=hid[:].rearrange("p c t -> p (c t)"))
            res = keep.tile([P, PACK, n], F32, name="res%d" % c0)
            per_bank = BANK // n
            for t0 in range(0, PACK, per_bank):
                obank = psum.tile([P, per_bank, n], F32, name="obank", tag="bank")
                for j in range(per_bank):
                    for a, b in PASSES[n]:
                        product(obank[:, j, a:b], 2, t0 + j, hq[:, a:b], hs[:, a:b])
                nc.scalar.copy(res[:, t0 : t0 + per_bank, :], obank[:])
            nc.sync.dma_start(out=out_rows[:, :, c0 : c0 + n], in_=res[:])
            rounded = keep.tile([P, n, PACK], BF16, name="rounded%d" % c0, align_bytes=64)
            (nc.scalar.copy if c0 == 0 else nc.vector.tensor_copy)(
                out=rounded[:].rearrange("p (c i) t -> p c t i", i=4),
                in_=res[:].rearrange("p t (c i) -> p c t i", i=4),
            )
            oq = keep.tile([P, n], U32, name="oq%d" % c0, align_bytes=64)
            nc.vector.quantize_mx(
                out=oq[:].bitcast(FP8X4), scales=out_scales[:, c0 : c0 + n], in_=rounded[:].rearrange("p c t -> p (c t)")
            )
            nc.sync.dma_start(out=out_words[:, c0 : c0 + n], in_=oq[:].bitcast(I32))

        c0 = 0
        for n in CHUNKS:
            dy, dz = gaps(c0, n)
            finish(c0, n, dy, dz)
            c0 = c0 + n

        for q in range(4):
            queue = nc.sync if q % 2 == 0 else nc.scalar
            queue.dma_start(out=out_2[0, 4 * q : 4 * q + 4, :].bitcast(I32), in_=out_scales[32 * q : 32 * q + 4, :].bitcast(I32))
